import numpy as np
import ml_dtypes


def mxq(x, axis, fmt="e4m3"):
    dtype, down = {"e4m3": (ml_dtypes.float8_e4m3fn, 7), "e5m2": (ml_dtypes.float8_e5m2, 14)}[fmt]
    v = np.moveaxis(np.asarray(x, np.float32).astype(ml_dtypes.bfloat16).astype(np.float64), axis, -1)
    blocks = v.reshape(v.shape[:-1] + (-1, 32))
    amax = np.abs(blocks).max(-1, keepdims=True)
    byte = np.maximum(np.where(amax > 0, np.frexp(amax)[1] - 1 + 127, 0) - down, 1)
    scale = np.exp2(byte - 127.0)
    codes = (blocks / scale).astype(np.float32).astype(dtype).astype(np.float64)
    return np.moveaxis((codes * scale).reshape(v.shape), -1, axis)


WIDE = False


def mx_kscale(k):
    if not WIDE:
        return np.ones(k)
    levels = np.array([10, -10, 5, -5, 0])
    if k % 512:
        return np.exp2(np.random.permutation(np.resize(levels, k // 32))).repeat(32)
    a = np.empty((k // 512, 16))
    for p in range(k // 512):
        a[p, :8] = np.random.permutation(np.resize(levels, 8))
        for g in range(8):
            far = levels[np.abs(levels - a[p, g]) >= 10]
            a[p, g + 8] = far[np.random.randint(len(far))]
    return np.exp2(a.ravel()).repeat(32)


def f64(x):
    return np.asarray(x).astype(np.float64)


def striped(idx):
    return np.tile(idx.reshape(-1, 16).T, (8, 1)).astype(np.uint16)


def unstriped(offs):
    return offs[:16].T.reshape(-1).astype(np.int64)


def striped8(idx):
    return np.concatenate([x.reshape(-1, 16).T for x in idx]).astype(np.uint16)


def runs(offs, k):
    lists = np.stack([offs[16 * r : 16 * r + 16].T.reshape(-1) for r in range(8)]).astype(np.int64)
    return lists[np.arange(k) % 512 // 64]


def pack_weight(w):
    k, n = w.shape
    w = f64(np.asarray(w, np.float32).astype(ml_dtypes.bfloat16)).reshape(k // 32, 32, n)
    amax = np.abs(w).max(1)
    byte = np.clip(np.where(amax > 0, np.frexp(amax)[1] - 1 + 127 - 7, 1), 1, 254)
    scaled = (w * np.exp2(127.0 - byte)[:, None, :]).reshape(k, n).astype(np.float32)
    words = np.ascontiguousarray(scaled.reshape(k // 512, 128, 4, n).transpose(0, 1, 3, 2)).astype(ml_dtypes.float8_e4m3fn).view(np.uint8)
    return words, np.ascontiguousarray(byte.astype(np.uint8).reshape(k // 512, 16, n))


def unpack_weight(words, scales):
    g, p, n, _ = words.shape
    vals = np.ascontiguousarray(words).view(ml_dtypes.float8_e4m3fn).astype(np.float64) * np.repeat(np.exp2(scales.astype(np.float64) - 127.0), 8, axis=1)[..., None]
    return vals.transpose(0, 1, 3, 2).reshape(g * 512, n)


E2M1 = np.array([0.0, 0.5, 1.0, 1.5, 2.0, 3.0, 4.0, 6.0, -0.0, -0.5, -1.0, -1.5, -2.0, -3.0, -4.0, -6.0])


def pack_fp4(w):
    k, n = w.shape
    w = f64(np.asarray(w, np.float32).astype(ml_dtypes.bfloat16)).reshape(k // 32, 32, n)
    amax = np.abs(w).max(1)
    mant, ex = np.frexp(amax / 6.0)
    byte = np.clip(np.where(amax > 0, np.where(mant > 0.5, ex, ex - 1) + 127, 1), 1, 254)
    scaled = (w * np.exp2(127.0 - byte)[:, None, :]).reshape(k, n).astype(np.float32)
    c = np.ascontiguousarray(scaled.reshape(k // 512, 128, 4, n).transpose(0, 1, 3, 2)).astype(ml_dtypes.float4_e2m1fn).view(np.uint8) & 0xF
    words = (c[..., 0::2] | (c[..., 1::2] << 4)).reshape(k // 512, 128, 2 * n)
    return np.ascontiguousarray(words), np.ascontiguousarray(byte.astype(np.uint8).reshape(k // 512, 16, n))


def unpack_fp4(words, scales):
    g, _, n = scales.shape
    words = np.ascontiguousarray(words).reshape(g, 128, n, 2)
    nib = np.empty((g, 128, n, 4), np.uint8)
    nib[..., 0::2] = words & 0xF
    nib[..., 1::2] = words >> 4
    vals = E2M1[nib] * np.repeat(np.exp2(scales.astype(np.float64) - 127.0), 8, axis=1)[..., None]
    return vals.transpose(0, 1, 3, 2).reshape(g * 512, n)


def sigmoid(v):
    return 1.0 / (1.0 + np.exp(-np.maximum(v, -700.0)))

def planes(y):
    n, m = y.shape
    v = y.astype(np.float32).astype(ml_dtypes.bfloat16).astype(np.float64).reshape(n // 32, 32, m)
    top = np.abs(v).max(1)
    byte = np.clip(np.where(top > 0, np.frexp(top)[1] - 1 + 127 - 7, 1), 1, 254)
    codes = (v * np.exp2(127.0 - byte)[:, None, :]).reshape(n, m).astype(np.float32).astype(ml_dtypes.float8_e4m3fn).view(np.uint8)
    words = codes.reshape(n // 512, 128, 4, m).transpose(0, 1, 3, 2)
    return np.ascontiguousarray(words), np.ascontiguousarray(byte.astype(np.uint8).reshape(n // 512, 16, m))


K, T, S, N, H = 512, 2048, 256, 512, 512


def setup_inputs():
    n = np.random.standard_normal
    s = mx_kscale(K)[:, None]
    u = mx_kscale(H)
    packed_xT = pack_weight(n((K, T)) * s)
    packed_w1 = pack_fp4(n((K, H)) / np.sqrt(K) / s)
    packed_w2 = pack_fp4(n((H, N)) / np.sqrt(H) / u[:, None])
    packed_w3 = pack_fp4(n((K, N)) / np.sqrt(K) / s)
    return {
        "x_words": packed_xT[0],
        "x_scales": packed_xT[1],
        "w1_words": packed_w1[0],
        "w1_scales": packed_w1[1],
        "sl": np.random.uniform(1.0, 2.0, (H, 1)).astype(np.float32),
        "th": (0.5 * n((H, 1))).astype(np.float32),
        "gn": (np.random.uniform(0.5, 1.5, (H, 1)) * u[:, None]).astype(np.float32),
        "w2_words": packed_w2[0],
        "w2_scales": packed_w2[1],
        "w3_words": packed_w3[0],
        "w3_scales": packed_w3[1],
        "offs": striped(np.random.permutation(T)[:S]),
        "n1": striped8(np.stack([np.random.permutation(S) for _ in range(8)])),
        "n2": striped8(np.stack([np.random.permutation(S) for _ in range(8)])),
        "two": striped(np.random.permutation(T)[:S]),
        "n3": striped(np.random.permutation(S)),
        "n4": striped(np.random.permutation(S)),
    }


def reference(x_words, x_scales, w1_words, w1_scales, sl, th, gn, w2_words, w2_scales, w3_words, w3_scales, offs, n1, n2, two, n3, n4):
    xq = unpack_weight(x_words, x_scales)[:, unstriped(offs)]
    y = unpack_fp4(w1_words, w1_scales).T @ xq
    sg = sigmoid(f64(sl) * (y[np.arange(H)[:, None], runs(n1, H)] - f64(th)))
    z = f64(gn) * (np.maximum(y * sg, 0.75 * (y[np.arange(H)[:, None], runs(n2, H)])))
    h = unpack_fp4(w2_words, w2_scales).T @ mxq(z, 0, "e4m3")
    x_two = unpack_weight(x_words, x_scales)[:, unstriped(two)]
    d = unpack_fp4(w3_words, w3_scales).T @ x_two
    out_0 = 0.75 * (h * d[:, unstriped(n4)] - (h[:, unstriped(n3)] * d))
    return (out_0,) + planes(out_0)

@@ -1,0 +1,243 @@
+from contextlib import ExitStack
+
+import concourse.mybir as mybir
+
+K, T, S, N, H = 512, 2048, 256, 512, 512
+FLOPS = 3 * 2 * 512 * 512 * 256
+
+F32 = mybir.dt.float32
+BF16 = mybir.dt.bfloat16
+I32 = mybir.dt.int32
+U32 = mybir.dt.uint32
+U16 = mybir.dt.uint16
+U8 = mybir.dt.uint8
+FP8X4 = mybir.dt.float8_e4m3fn_x4
+FP4X4 = mybir.dt.float4_e2m1fn_x4
+MULT = mybir.AluOpType.mult
+ADD = mybir.AluOpType.add
+MAX = mybir.AluOpType.max
+SUB = mybir.AluOpType.subtract
+SIGMOID = mybir.ActivationFunctionType.Sigmoid
+COPY = mybir.ActivationFunctionType.Copy
+
+P = 128
+PACK = 4
+HALF = S // 2
+LIST_COLS = S // 16
+
+
+def tile_picked_latecrossbemo_none_po_kernel(
+    tc, x_words, x_scales, w1_words, w1_scales, sl, th, gn, w2_words, w2_scales, w3_words, w3_scales,
+    offs, n1, n2, two, n3, n4, out_0, out_1, out_2,
+):
+    nc = tc.nc
+    with ExitStack() as ctx:
+        keep = ctx.enter_context(tc.tile_pool(name="keep", bufs=1))
+        psum = ctx.enter_context(tc.psum_pool(name="psum", bufs=1))
+
+        def sb(name, shape, dtype, tag=None):
+            return keep.tile(shape, dtype, name=name, tag=tag or name, align_bytes=64)
+
+        def load_list(name, src):
+            t = keep.tile([P, LIST_COLS], U16, name=name)
+            nc.sync.dma_start(t[:], src)
+            return t
+
+        def load_scale_rows(queues, dst, src):
+            for q in range(4):
+                queues[q].dma_start(dst[32 * q : 32 * q + 4, :].bitcast(I32), src[0, 4 * q : 4 * q + 4, :].bitcast(I32))
+
+        def load_words(queue, name, src):
+            t = sb(name, [P, H // 2], I32)
+            queue.dma_start(t[:], src[0].bitcast(I32))
+            return t
+
+        def load_rows(name, src):
+            t = sb(name, [P, PACK], F32)
+            nc.gpsimd.dma_start(t[:], src.rearrange("(p t) o -> p (t o)", t=PACK))
+            return t
+
+        def deal_words(name, raw):
+            t = sb(name, [P, 2 * H], U8)
+            nc.scalar.copy(
+                t[:].bitcast(U16).rearrange("p (t m) -> p t m", t=PACK),
+                raw[:].bitcast(U16).rearrange("p (m t) -> p t m", t=PACK),
+            )
+            return t
+
+        def deal_scales(name, raw):
+            t = sb(name, [P, H], U8)
+            nc.vector.tensor_copy(
+                t[:].rearrange("p (t m) -> p t m", t=PACK),
+                raw.rearrange("p (m t) -> p t m", t=PACK),
+            )
+            return t
+
+        def half_list(lst, c):
+            return lst[:, c * (LIST_COLS // 2) : (c + 1) * (LIST_COLS // 2)]
+
+        def product(out, words, scales, t, rhs_words, rhs_scales):
+            nc.tensor.matmul_mx(
+                out=out,
+                lhsT=words[:, 2 * P * t : 2 * P * (t + 1)].bitcast(FP4X4),
+                lhsT_scale=scales[:, P * t : P * (t + 1)],
+                rhs=rhs_words.bitcast(FP8X4),
+                rhs_scale=rhs_scales,
+                start=True,
+                stop=True,
+            )
+
+        xs = sb("xs", [P, T], U8)
+        nc.vector.memset(xs[:].bitcast(I32), 0)
+        ws_raw = sb("ws_raw", [P, 3 * H], U8)
+        nc.vector.memset(ws_raw[:].bitcast(I32), 0)
+        w1s_raw = ws_raw[:, 0:H]
+        w3s_raw = ws_raw[:, H : 2 * H]
+        w2s_raw = ws_raw[:, 2 * H : 3 * H]
+
+        xs_stage = sb("xs_stage", [P, T], U8)
+        w1s_stage = sb("w1s_stage", [P, H], U8)
+        offs_t = load_list("offs_t", offs)
+        load_scale_rows([nc.scalar] * 4, xs_stage, x_scales)
+        two_t = load_list("two_t", two)
+        w1w_raw = load_words(nc.sync, "w1w_raw", w1_words)
+        xw = sb("xw", [P, T], I32)
+        nc.sync.dma_start(xw[:], x_words[0].rearrange("p n t -> p (n t)").bitcast(I32))
+        load_scale_rows([nc.scalar] * 4, w1s_stage, w1_scales)
+        w3w_raw = load_words(nc.sync, "w3w_raw", w3_words)
+        n1_t = load_list("n1_t", n1)
+        n2_t = load_list("n2_t", n2)
+        n4_t = load_list("n4_t", n4)
+        n3_t = load_list("n3_t", n3)
+        w2w_raw = load_words(nc.gpsimd, "w2w_raw", w2_words)
+        sl_t = load_rows("sl_t", sl)
+        th_t = load_rows("th_t", th)
+        slth = sb("slth", [P, PACK], F32)
+        nc.gpsimd.tensor_tensor(slth[:], sl_t[:], th_t[:], MULT)
+        bias = sb("bias", [P, PACK], F32)
+        nc.gpsimd.tensor_scalar(bias[:], slth[:], -1.0, 0.0, MULT, ADD)
+        gn_t = load_rows("gn_t", gn)
+        load_scale_rows([nc.sync] * 4, w3s_raw, w3_scales)
+        load_scale_rows([nc.sync] * 4, w2s_raw, w2_scales)
+        ds = sb("ds", [P, PACK + 1, S], F32)
+        nc.gpsimd.memset(ds[:, PACK, :], 0.0)
+        h = [sb("h%d" % t, [P, S + 16], F32) for t in range(PACK)]
+        for t in range(PACK):
+            nc.gpsimd.memset(h[t][:, S:], 0.0)
+
+        for q in range(4):
+            rows = slice(32 * q, 32 * q + 4)
+            nc.vector.tensor_copy(xs[rows, :].bitcast(I32), xs_stage[rows, :].bitcast(I32))
+        w1w = deal_words("w1w", w1w_raw)
+        for q in range(4):
+            rows = slice(32 * q, 32 * q + 4)
+            nc.scalar.copy(w1s_raw[rows, :].bitcast(U32), w1s_stage[rows, :].bitcast(U32))
+        xa_s = sb("xa_s", [P, S], U8)
+        nc.vector.tensor_copy(xa_s[:], xs[:].indirect(offs_t[:]))
+        xa_w = sb("xa_w", [P, S], U32)
+        nc.vector.tensor_copy(xa_w[:], xw[:].bitcast(U32).indirect(offs_t[:]))
+        w1s = deal_scales("w1s", w1s_raw)
+
+        y_ps = [psum.tile([P, S], F32, name="y_ps%d" % t, tag="bank%d" % t) for t in range(PACK)]
+        for t in range(PACK):
+            product(y_ps[t][:], w1w, w1s, t, xa_w[:], xa_s[:])
+
+        xb_s = sb("xb_s", [P, S], U8)
+        nc.vector.tensor_copy(xb_s[:], xs[:].indirect(two_t[:]))
+        xb_w = sb("xb_w", [P, S], U32)
+        nc.vector.tensor_copy(xb_w[:], xw[:].bitcast(U32).indirect(two_t[:]))
+
+        y = [sb("y%d" % t, [P, S], F32) for t in range(PACK)]
+        for t in range(PACK):
+            nc.vector.tensor_copy(y[t][:], y_ps[t][:])
+
+        w3w = deal_words("w3w", w3w_raw)
+        w2w = deal_words("w2w", w2w_raw)
+        w3s = deal_scales("w3s", w3s_raw)
+        w2s = deal_scales("w2s", w2s_raw)
+        d_ps = [psum.tile([P, 2, S], F32, name="d_ps%d" % u, tag="bank%d" % (4 + u)) for u in range(2)]
+        for t in range(PACK):
+            product(d_ps[t // 2][:, t % 2, :], w3w, w3s, t, xb_w[:], xb_s[:])
+        for u in range(2):
+            nc.vector.tensor_scalar(ds[:, 2 * u : 2 * u + 2, :], d_ps[u][:], 0.75, None, MULT)
+
+        ha_ps = psum.tile([P, PACK, HALF], F32, name="ha_ps", tag="bank6")
+        hb_ps = [psum.tile([P, 2, HALF], F32, name="hb_ps%d" % u, tag="bank%d" % u) for u in range(2)]
+        for c in range(2):
+            cols = slice(c * HALF, (c + 1) * HALF)
+            sg = sb("sg%d" % c, [P, PACK, HALF], F32)
+            y2 = sb("y2_%d" % c, [P, PACK, HALF], F32)
+            ysg = sb("ysg%d" % c, [P, PACK, HALF], F32, tag="ysg0" if c == 0 else "top0")
+            top = sb("top%d" % c, [P, PACK, HALF], F32)
+            for t in range(PACK):
+                nc.scalar.activation(
+                    sg[:, t, :], y[t][:].indirect(half_list(n1_t, c)), SIGMOID,
+                    bias=bias[:, t : t + 1], scale=sl_t[:, t : t + 1],
+                )
+                if c == 0:
+                    nc.scalar.activation(y2[:, t, :], y[t][:].indirect(half_list(n2_t, c)), COPY)
+            if c == 1:
+                for t in range(PACK):
+                    nc.scalar.activation(y2[:, t, :], y[t][:].indirect(half_list(n2_t, c)), COPY)
+            for t in range(PACK):
+                nc.vector.tensor_tensor(ysg[:, t, :], y[t][:, cols], sg[:, t, :], MULT)
+            for rows in ([slice(0, 4)] if c == 0 else [slice(0, 3), slice(3, 4)]):
+                nc.vector.scalar_tensor_tensor(top[:, rows, :], y2[:, rows, :], 0.75, ysg[:, rows, :], MULT, MAX)
+            zb = sb("zb%d" % c, [P, HALF, PACK], BF16)
+            nc.vector.tensor_tensor(
+                zb[:], top[:].rearrange("p t n -> p n t"),
+                gn_t[:].unsqueeze(1).to_broadcast([P, HALF, PACK]), MULT,
+            )
+            z_w = sb("z_w%d" % c, [P, HALF], U32)
+            z_s = sb("z_s%d" % c, [P, HALF], U8)
+            nc.vector.quantize_mx(z_w[:].bitcast(FP8X4), z_s[:], zb[:].rearrange("p n t -> p (n t)"))
+            for t in range(PACK):
+                dst = ha_ps[:, t, :] if c == 0 else hb_ps[t // 2][:, t % 2, :]
+                product(dst, w2w, w2s, t, z_w[:], z_s[:])
+
+        first, second = slice(0, HALF), slice(HALF, S)
+        for t in range(PACK):
+            nc.vector.tensor_copy(h[t][:, first], ha_ps[:, t, :])
+        d4 = sb("d4", [P, PACK, S], F32)
+        for t in range(PACK):
+            window = ds[:, t : t + 2, :].rearrange("p t n -> p (t n)")
+            nc.scalar.activation(d4[:, t, :], window.indirect(n4_t[:]), COPY)
+        hd = sb("hd", [P, PACK, S], F32, tag="zb1")
+        for pair in (slice(0, 2), slice(2, 4)):
+            nc.vector.tensor_tensor(hd[:, pair, first], ha_ps[:, pair, :], d4[:, pair, first], MULT)
+
+        h3 = sb("h3", [P, PACK - 1, S], F32)
+        h3d = sb("h3d", [P, PACK, S], F32)
+        res = sb("res", [P, PACK, S], F32)
+        out_rows = out_0.rearrange("(p t) n -> p t n", t=PACK)
+        nc.vector.tensor_copy(h[3][:, second], hb_ps[1][:, 1, :])
+        nc.scalar.copy(h[0][:, second], hb_ps[0][:, 0, :])
+        nc.scalar.copy(h[1][:, second], hb_ps[0][:, 1, :])
+        nc.vector.tensor_tensor(hd[:, 2:4, second], hb_ps[1][:], d4[:, 2:4, second], MULT)
+        nc.scalar.activation(h3[:, 0, :], h[0][:].indirect(n3_t[:]), COPY)
+        nc.scalar.copy(h[2][:, second], hb_ps[1][:, 0, :])
+        nc.scalar.activation(h3[:, 1, :], h[1][:].indirect(n3_t[:]), COPY)
+        nc.scalar.activation(h3[:, 2, :], h[2][:].indirect(n3_t[:]), COPY)
+        nc.vector.tensor_tensor(h3d[:, 3, :], h[3][:].indirect(n3_t[:]), ds[:, 3, :], MULT)
+        nc.vector.tensor_tensor(hd[:, 0:2, second], hb_ps[0][:], d4[:, 0:2, second], MULT)
+        for t in (3, 0, 1, 2):
+            if t < 3:
+                nc.vector.tensor_tensor(h3d[:, t, :], h3[:, t, :], ds[:, t, :], MULT)
+            nc.vector.tensor_tensor(res[:, t, :], hd[:, t, :], h3d[:, t, :], SUB)
+            nc.sync.dma_start(out_rows[:, t, :], res[:, t, :])
+
+        o_w = sb("o_w", [P, S], U32)
+        o_s = sb("o_s", [P, S], U8)
+        out_words = out_1[0].rearrange("p n t -> p (n t)").bitcast(I32)
+        ob = [sb("ob%d" % c, [P, HALF, PACK], BF16) for c in range(2)]
+        for c, cols in enumerate((first, second)):
+            nc.vector.tensor_copy(
+                ob[c][:].rearrange("p (a i) t -> p a t i", i=4),
+                res[:, :, cols].rearrange("p t (a i) -> p a t i", i=4),
+            )
+        for c, cols in enumerate((first, second)):
+            nc.vector.quantize_mx(o_w[:, cols].bitcast(FP8X4), o_s[:, cols], ob[c][:].rearrange("p n t -> p (n t)"))
+        nc.sync.dma_start(out_words, o_w[:].bitcast(I32))
+        for q in range(4):
+            queue = nc.sync if q % 2 == 1 else nc.scalar
+            queue.dma_start(out_2[0, 4 * q : 4 * q + 4, :].bitcast(I32), o_s[32 * q : 32 * q + 4, :].bitcast(I32))

@@ -45,7 +45,7 @@ def tile_picked_latecrossbemo_none_po_kernel(
 
         def load_scale_rows(queues, dst, src):
             for q in range(4):
-                queues[q].dma_start(dst[32 * q : 32 * q + 4, :].bitcast(I32), src[0, 4 * q : 4 * q + 4, :].bitcast(I32))
+                queues[q].dma_start(dst[q][32 * q : 32 * q + 4, :].bitcast(I32), src[0, 4 * q : 4 * q + 4, :].bitcast(I32))
 
         def load_words(queue, name, src):
             t = sb(name, [P, H // 2], I32)
@@ -65,9 +65,9 @@ def tile_picked_latecrossbemo_none_po_kernel(
             )
             return t
 
-        def deal_scales(name, raw):
+        def deal_scales(name, raw, engine):
             t = sb(name, [P, H], U8)
-            nc.vector.tensor_copy(
+            engine.tensor_copy(
                 t[:].rearrange("p (t m) -> p t m", t=PACK),
                 raw.rearrange("p (m t) -> p t m", t=PACK),
             )
@@ -89,27 +89,26 @@ def tile_picked_latecrossbemo_none_po_kernel(
 
         xs = sb("xs", [P, T], U8)
         nc.vector.memset(xs[:].bitcast(I32), 0)
-        ws_raw = sb("ws_raw", [P, 3 * H], U8)
-        nc.vector.memset(ws_raw[:].bitcast(I32), 0)
-        w1s_raw = ws_raw[:, 0:H]
-        w3s_raw = ws_raw[:, H : 2 * H]
-        w2s_raw = ws_raw[:, 2 * H : 3 * H]
+        w1s_raw = sb("w1s_raw", [P, H], U8)
+        nc.vector.memset(w1s_raw[:].bitcast(I32), 0)
+        w3s_raw = sb("w3s_raw", [P, N], U8)
+        w2s_raw = sb("w2s_raw", [P, N], U8)
+        nc.vector.memset(w3s_raw[:].bitcast(I32), 0)
+        nc.vector.memset(w2s_raw[:].bitcast(I32), 0)
 
         xs_stage = sb("xs_stage", [P, T], U8)
         w1s_stage = sb("w1s_stage", [P, H], U8)
+        load_scale_rows([nc.sync] * 4, [xs_stage] * 4, x_scales)
         offs_t = load_list("offs_t", offs)
-        load_scale_rows([nc.scalar] * 4, xs_stage, x_scales)
-        two_t = load_list("two_t", two)
-        w1w_raw = load_words(nc.sync, "w1w_raw", w1_words)
+        load_scale_rows([nc.sync] * 2 + [nc.gpsimd] * 2, [w1s_stage] * 4, w1_scales)
         xw = sb("xw", [P, T], I32)
         nc.sync.dma_start(xw[:], x_words[0].rearrange("p n t -> p (n t)").bitcast(I32))
-        load_scale_rows([nc.scalar] * 4, w1s_stage, w1_scales)
-        w3w_raw = load_words(nc.sync, "w3w_raw", w3_words)
+        w1w_raw = load_words(nc.sync, "w1w_raw", w1_words)
+        two_t = load_list("two_t", two)
         n1_t = load_list("n1_t", n1)
+        w3w_raw = load_words(nc.sync, "w3w_raw", w3_words)
+        w2w_raw = load_words(nc.sync, "w2w_raw", w2_words)
         n2_t = load_list("n2_t", n2)
-        n4_t = load_list("n4_t", n4)
-        n3_t = load_list("n3_t", n3)
-        w2w_raw = load_words(nc.gpsimd, "w2w_raw", w2_words)
         sl_t = load_rows("sl_t", sl)
         th_t = load_rows("th_t", th)
         slth = sb("slth", [P, PACK], F32)
@@ -117,18 +116,19 @@ def tile_picked_latecrossbemo_none_po_kernel(
         bias = sb("bias", [P, PACK], F32)
         nc.gpsimd.tensor_scalar(bias[:], slth[:], -1.0, 0.0, MULT, ADD)
         gn_t = load_rows("gn_t", gn)
-        load_scale_rows([nc.sync] * 4, w3s_raw, w3_scales)
-        load_scale_rows([nc.sync] * 4, w2s_raw, w2_scales)
+        load_scale_rows([nc.sync] * 4, [w3s_raw] * 4, w3_scales)
+        load_scale_rows([nc.sync] * 4, [w2s_raw] * 4, w2_scales)
+        n4_t = load_list("n4_t", n4)
+        n3_t = load_list("n3_t", n3)
         ds = sb("ds", [P, PACK + 1, S], F32)
-        nc.gpsimd.memset(ds[:, PACK, :], 0.0)
+        nc.vector.memset(ds[:, PACK, :], 0.0)
         h = [sb("h%d" % t, [P, S + 16], F32) for t in range(PACK)]
         for t in range(PACK):
-            nc.gpsimd.memset(h[t][:, S:], 0.0)
+            nc.scalar.copy(h[t][:, S:], ds[:, PACK, 0:16])
 
         for q in range(4):
             rows = slice(32 * q, 32 * q + 4)
             nc.vector.tensor_copy(xs[rows, :].bitcast(I32), xs_stage[rows, :].bitcast(I32))
-        w1w = deal_words("w1w", w1w_raw)
         for q in range(4):
             rows = slice(32 * q, 32 * q + 4)
             nc.scalar.copy(w1s_raw[rows, :].bitcast(U32), w1s_stage[rows, :].bitcast(U32))
@@ -136,37 +136,43 @@ def tile_picked_latecrossbemo_none_po_kernel(
         nc.vector.tensor_copy(xa_s[:], xs[:].indirect(offs_t[:]))
         xa_w = sb("xa_w", [P, S], U32)
         nc.vector.tensor_copy(xa_w[:], xw[:].bitcast(U32).indirect(offs_t[:]))
-        w1s = deal_scales("w1s", w1s_raw)
+        w1s = sb("w1s", [P, H], U8)
+        for t in range(PACK):
+            nc.vector.tensor_copy(w1s[:, P * t : P * (t + 1)], w1s_raw[:, t:H:PACK])
+        w1w = sb("w1w", [P, 2 * H], U8)
+        for t in range(PACK):
+            nc.scalar.copy(w1w[:, 2 * P * t : 2 * P * (t + 1)].bitcast(U16), w1w_raw[:].bitcast(U16)[:, t:H:PACK])
 
         y_ps = [psum.tile([P, S], F32, name="y_ps%d" % t, tag="bank%d" % t) for t in range(PACK)]
         for t in range(PACK):
             product(y_ps[t][:], w1w, w1s, t, xa_w[:], xa_s[:])
 
-        xb_s = sb("xb_s", [P, S], U8)
-        nc.vector.tensor_copy(xb_s[:], xs[:].indirect(two_t[:]))
         xb_w = sb("xb_w", [P, S], U32)
         nc.vector.tensor_copy(xb_w[:], xw[:].bitcast(U32).indirect(two_t[:]))
 
         y = [sb("y%d" % t, [P, S], F32) for t in range(PACK)]
-        for t in range(PACK):
+        nc.scalar.copy(y[0][:], y_ps[0][:])
+        for t in range(1, PACK):
             nc.vector.tensor_copy(y[t][:], y_ps[t][:])
 
+        xb_s = sb("xb_s", [P, S], U8)
+        nc.vector.tensor_copy(xb_s[:], xs[:].indirect(two_t[:]))
         w3w = deal_words("w3w", w3w_raw)
         w2w = deal_words("w2w", w2w_raw)
-        w3s = deal_scales("w3s", w3s_raw)
-        w2s = deal_scales("w2s", w2s_raw)
+        w3s = deal_scales("w3s", w3s_raw[:], nc.gpsimd)
+        w2s = deal_scales("w2s", w2s_raw[:], nc.gpsimd)
         d_ps = [psum.tile([P, 2, S], F32, name="d_ps%d" % u, tag="bank%d" % (4 + u)) for u in range(2)]
         for t in range(PACK):
             product(d_ps[t // 2][:, t % 2, :], w3w, w3s, t, xb_w[:], xb_s[:])
         for u in range(2):
             nc.vector.tensor_scalar(ds[:, 2 * u : 2 * u + 2, :], d_ps[u][:], 0.75, None, MULT)
 
-        ha_ps = psum.tile([P, PACK, HALF], F32, name="ha_ps", tag="bank6")
-        hb_ps = [psum.tile([P, 2, HALF], F32, name="hb_ps%d" % u, tag="bank%d" % u) for u in range(2)]
+        sg = sb("sg", [P, PACK, HALF], F32, tag="w3w_raw")
+        y2 = sb("y_n2", [P, PACK, HALF], F32, tag="w2w_raw")
+        ha_ps = [psum.tile([P, 2, HALF], F32, name="ha_ps%d" % u, tag="bank%d" % (4 + u)) for u in range(2)]
+        hb_ps = [psum.tile([P, 2, HALF], F32, name="hb_ps%d" % u, tag="bank%d" % (6 + u)) for u in range(2)]
         for c in range(2):
             cols = slice(c * HALF, (c + 1) * HALF)
-            sg = sb("sg%d" % c, [P, PACK, HALF], F32)
-            y2 = sb("y2_%d" % c, [P, PACK, HALF], F32)
             ysg = sb("ysg%d" % c, [P, PACK, HALF], F32, tag="ysg0" if c == 0 else "top0")
             top = sb("top%d" % c, [P, PACK, HALF], F32)
             for t in range(PACK):
@@ -180,7 +186,7 @@ def tile_picked_latecrossbemo_none_po_kernel(
                 for t in range(PACK):
                     nc.scalar.activation(y2[:, t, :], y[t][:].indirect(half_list(n2_t, c)), COPY)
             for t in range(PACK):
-                nc.vector.tensor_tensor(ysg[:, t, :], y[t][:, cols], sg[:, t, :], MULT)
+                nc.vector.tensor_tensor(ysg[:, t, :], y_ps[t][:, cols], sg[:, t, :], MULT)
             for rows in ([slice(0, 4)] if c == 0 else [slice(0, 3), slice(3, 4)]):
                 nc.vector.scalar_tensor_tensor(top[:, rows, :], y2[:, rows, :], 0.75, ysg[:, rows, :], MULT, MAX)
             zb = sb("zb%d" % c, [P, HALF, PACK], BF16)
@@ -192,19 +198,20 @@ def tile_picked_latecrossbemo_none_po_kernel(
             z_s = sb("z_s%d" % c, [P, HALF], U8)
             nc.vector.quantize_mx(z_w[:].bitcast(FP8X4), z_s[:], zb[:].rearrange("p n t -> p (n t)"))
             for t in range(PACK):
-                dst = ha_ps[:, t, :] if c == 0 else hb_ps[t // 2][:, t % 2, :]
+                dst = (ha_ps, hb_ps)[c][t // 2][:, t % 2, :]
                 product(dst, w2w, w2s, t, z_w[:], z_s[:])
 
         first, second = slice(0, HALF), slice(HALF, S)
         for t in range(PACK):
-            nc.vector.tensor_copy(h[t][:, first], ha_ps[:, t, :])
+            nc.vector.tensor_copy(h[t][:, first], ha_ps[t // 2][:, t % 2, :])
         d4 = sb("d4", [P, PACK, S], F32)
         for t in range(PACK):
             window = ds[:, t : t + 2, :].rearrange("p t n -> p (t n)")
             nc.scalar.activation(d4[:, t, :], window.indirect(n4_t[:]), COPY)
         hd = sb("hd", [P, PACK, S], F32, tag="zb1")
-        for pair in (slice(0, 2), slice(2, 4)):
-            nc.vector.tensor_tensor(hd[:, pair, first], ha_ps[:, pair, :], d4[:, pair, first], MULT)
+        for u in range(2):
+            pair = slice(2 * u, 2 * u + 2)
+            nc.vector.tensor_tensor(hd[:, pair, first], ha_ps[u][:], d4[:, pair, first], MULT)
 
         h3 = sb("h3", [P, PACK - 1, S], F32)
         h3d = sb("h3d", [P, PACK, S], F32)

@@ -43,9 +43,9 @@ def tile_picked_latecrossbemo_none_po_kernel(
             nc.sync.dma_start(t[:], src)
             return t
 
-        def load_scale_rows(queues, dst, src):
-            for q in range(4):
-                queues[q].dma_start(dst[q][32 * q : 32 * q + 4, :].bitcast(I32), src[0, 4 * q : 4 * q + 4, :].bitcast(I32))
+        def load_scale_rows(dst, src, quadrants=range(4)):
+            for q in quadrants:
+                nc.sync.dma_start(dst[32 * q : 32 * q + 4, :].bitcast(I32), src[0, 4 * q : 4 * q + 4, :].bitcast(I32))
 
         def load_words(queue, name, src):
             t = sb(name, [P, H // 2], I32)
@@ -76,6 +76,9 @@ def tile_picked_latecrossbemo_none_po_kernel(
         def half_list(lst, c):
             return lst[:, c * (LIST_COLS // 2) : (c + 1) * (LIST_COLS // 2)]
 
+        def two_rows(tile, t):
+            return tile[:, t : t + 2, :].rearrange("p t n -> p (t n)")
+
         def product(out, words, scales, t, rhs_words, rhs_scales):
             nc.tensor.matmul_mx(
                 out=out,
@@ -98,11 +101,12 @@ def tile_picked_latecrossbemo_none_po_kernel(
 
         xs_stage = sb("xs_stage", [P, T], U8)
         w1s_stage = sb("w1s_stage", [P, H], U8)
-        load_scale_rows([nc.sync] * 4, [xs_stage] * 4, x_scales)
+        load_scale_rows(xs_stage, x_scales)
         offs_t = load_list("offs_t", offs)
-        load_scale_rows([nc.sync] * 2 + [nc.gpsimd] * 2, [w1s_stage] * 4, w1_scales)
+        load_scale_rows(w1s_stage, w1_scales, (0, 1))
         xw = sb("xw", [P, T], I32)
         nc.sync.dma_start(xw[:], x_words[0].rearrange("p n t -> p (n t)").bitcast(I32))
+        load_scale_rows(w1s_stage, w1_scales, (2, 3))
         w1w_raw = load_words(nc.sync, "w1w_raw", w1_words)
         two_t = load_list("two_t", two)
         n1_t = load_list("n1_t", n1)
@@ -116,15 +120,19 @@ def tile_picked_latecrossbemo_none_po_kernel(
         bias = sb("bias", [P, PACK], F32)
         nc.gpsimd.tensor_scalar(bias[:], slth[:], -1.0, 0.0, MULT, ADD)
         gn_t = load_rows("gn_t", gn)
-        load_scale_rows([nc.sync] * 4, [w3s_raw] * 4, w3_scales)
-        load_scale_rows([nc.sync] * 4, [w2s_raw] * 4, w2_scales)
+        load_scale_rows(w3s_raw, w3_scales)
+        load_scale_rows(w2s_raw, w2_scales)
         n4_t = load_list("n4_t", n4)
         n3_t = load_list("n3_t", n3)
         ds = sb("ds", [P, PACK + 1, S], F32)
         nc.vector.memset(ds[:, PACK, :], 0.0)
-        h = [sb("h%d" % t, [P, S + 16], F32) for t in range(PACK)]
+        h = sb("h", [P, PACK, S], F32)
+        nc.scalar.copy(h[:, PACK - 1, :], ds[:, PACK, :])
+        h_last = sb("h_last", [P, S + 16], F32)
+        nc.scalar.copy(h_last[:, S:], ds[:, PACK, 0:16])
+        y = [sb("y%d" % t, [P, 2 * S], F32) for t in range(PACK)]
         for t in range(PACK):
-            nc.scalar.copy(h[t][:, S:], ds[:, PACK, 0:16])
+            nc.scalar.copy(y[t][:, S:], ds[:, PACK, :])
 
         for q in range(4):
             rows = slice(32 * q, 32 * q + 4)
@@ -150,64 +158,74 @@ def tile_picked_latecrossbemo_none_po_kernel(
         xb_w = sb("xb_w", [P, S], U32)
         nc.vector.tensor_copy(xb_w[:], xw[:].bitcast(U32).indirect(two_t[:]))
 
-        y = [sb("y%d" % t, [P, S], F32) for t in range(PACK)]
-        nc.scalar.copy(y[0][:], y_ps[0][:])
-        for t in range(1, PACK):
-            nc.vector.tensor_copy(y[t][:], y_ps[t][:])
+        for t in range(PACK):
+            nc.vector.tensor_copy(y[t][:, 0:S], y_ps[t][:])
 
         xb_s = sb("xb_s", [P, S], U8)
         nc.vector.tensor_copy(xb_s[:], xs[:].indirect(two_t[:]))
         w3w = deal_words("w3w", w3w_raw)
         w2w = deal_words("w2w", w2w_raw)
-        w3s = deal_scales("w3s", w3s_raw[:], nc.gpsimd)
-        w2s = deal_scales("w2s", w2s_raw[:], nc.gpsimd)
+        w3s = deal_scales("w3s", w3s_raw[:], nc.vector)
+        w2s = deal_scales("w2s", w2s_raw[:], nc.vector)
         d_ps = [psum.tile([P, 2, S], F32, name="d_ps%d" % u, tag="bank%d" % (4 + u)) for u in range(2)]
         for t in range(PACK):
             product(d_ps[t // 2][:, t % 2, :], w3w, w3s, t, xb_w[:], xb_s[:])
         for u in range(2):
             nc.vector.tensor_scalar(ds[:, 2 * u : 2 * u + 2, :], d_ps[u][:], 0.75, None, MULT)
 
-        sg = sb("sg", [P, PACK, HALF], F32, tag="w3w_raw")
-        y2 = sb("y_n2", [P, PACK, HALF], F32, tag="w2w_raw")
+        first, second = slice(0, HALF), slice(HALF, S)
+        sg = sb("sg", [P, PACK, S], F32, tag="w3w_raw")
+        y2 = sb("y_n2", [P, PACK, S], F32, tag="w2w_raw")
+        ysg = sb("ysg", [P, PACK, S], F32, tag="w3s_raw")
+        top = sb("top", [P, PACK, S], F32, tag="w3s")
+
+        def gate(t):
+            nc.scalar.activation(
+                sg[:, t, :], y[t][:].indirect(n1_t[:]), SIGMOID, bias=bias[:, t : t + 1], scale=sl_t[:, t : t + 1]
+            )
+            nc.vector.tensor_tensor(ysg[:, t, :], y[t][:, 0:S], sg[:, t, :], MULT)
+
+        def larger(t, offsets, cols):
+            nc.scalar.activation(y2[:, t, cols], y[t][:].indirect(offsets), COPY)
+            nc.vector.scalar_tensor_tensor(top[:, t, cols], y2[:, t, cols], 0.75, ysg[:, t, cols], MULT, MAX)
+
+        for t in (0, 1):
+            gate(t)
+            larger(t, n2_t[:], slice(0, S))
+        for t in (2, 3):
+            gate(t)
+
         ha_ps = [psum.tile([P, 2, HALF], F32, name="ha_ps%d" % u, tag="bank%d" % (4 + u)) for u in range(2)]
-        hb_ps = [psum.tile([P, 2, HALF], F32, name="hb_ps%d" % u, tag="bank%d" % (6 + u)) for u in range(2)]
-        for c in range(2):
-            cols = slice(c * HALF, (c + 1) * HALF)
-            ysg = sb("ysg%d" % c, [P, PACK, HALF], F32, tag="ysg0" if c == 0 else "top0")
-            top = sb("top%d" % c, [P, PACK, HALF], F32)
-            for t in range(PACK):
-                nc.scalar.activation(
-                    sg[:, t, :], y[t][:].indirect(half_list(n1_t, c)), SIGMOID,
-                    bias=bias[:, t : t + 1], scale=sl_t[:, t : t + 1],
-                )
-                if c == 0:
-                    nc.scalar.activation(y2[:, t, :], y[t][:].indirect(half_list(n2_t, c)), COPY)
-            if c == 1:
-                for t in range(PACK):
-                    nc.scalar.activation(y2[:, t, :], y[t][:].indirect(half_list(n2_t, c)), COPY)
-            for t in range(PACK):
-                nc.vector.tensor_tensor(ysg[:, t, :], y_ps[t][:, cols], sg[:, t, :], MULT)
-            for rows in ([slice(0, 4)] if c == 0 else [slice(0, 3), slice(3, 4)]):
-                nc.vector.scalar_tensor_tensor(top[:, rows, :], y2[:, rows, :], 0.75, ysg[:, rows, :], MULT, MAX)
-            zb = sb("zb%d" % c, [P, HALF, PACK], BF16)
+        hb01_ps = psum.tile([P, 2, HALF], F32, name="hb01_ps", tag="bank6")
+        hb2_ps = psum.tile([P, HALF], F32, name="hb2_ps", tag="bank7")
+        hb3_ps = psum.tile([P, HALF], F32, name="hb3_ps", tag="bank0")
+        h_dst = [
+            [(t, ha_ps[t // 2][:, t % 2, :]) for t in range(PACK)],
+            [(3, hb3_ps[:]), (0, hb01_ps[:, 0, :]), (1, hb01_ps[:, 1, :]), (2, hb2_ps[:])],
+        ]
+        gain = gn_t[:].unsqueeze(1).unsqueeze(3).to_broadcast([P, HALF // 4, PACK, 4])
+        for c, cols in enumerate((first, second)):
+            for t in (2, 3):
+                larger(t, half_list(n2_t, c), cols)
+            zb = sb("zb%d" % c, [P, HALF, PACK], BF16, tag="w2s_raw" if c == 0 else "zb1")
             nc.vector.tensor_tensor(
-                zb[:], top[:].rearrange("p t n -> p n t"),
-                gn_t[:].unsqueeze(1).to_broadcast([P, HALF, PACK]), MULT,
+                zb[:].rearrange("p (a i) t -> p a t i", i=4),
+                top[:, :, cols].rearrange("p t (a i) -> p a t i", i=4),
+                gain,
+                MULT,
             )
             z_w = sb("z_w%d" % c, [P, HALF], U32)
             z_s = sb("z_s%d" % c, [P, HALF], U8)
             nc.vector.quantize_mx(z_w[:].bitcast(FP8X4), z_s[:], zb[:].rearrange("p n t -> p (n t)"))
-            for t in range(PACK):
-                dst = (ha_ps, hb_ps)[c][t // 2][:, t % 2, :]
+            for t, dst in h_dst[c]:
                 product(dst, w2w, w2s, t, z_w[:], z_s[:])
 
-        first, second = slice(0, HALF), slice(HALF, S)
-        for t in range(PACK):
-            nc.vector.tensor_copy(h[t][:, first], ha_ps[t // 2][:, t % 2, :])
         d4 = sb("d4", [P, PACK, S], F32)
         for t in range(PACK):
-            window = ds[:, t : t + 2, :].rearrange("p t n -> p (t n)")
-            nc.scalar.activation(d4[:, t, :], window.indirect(n4_t[:]), COPY)
+            nc.scalar.activation(d4[:, t, :], two_rows(ds, t).indirect(n4_t[:]), COPY)
+        nc.vector.tensor_copy(h_last[:, first], ha_ps[1][:, 1, :])
+        nc.scalar.copy(h[:, 0:2, first], ha_ps[0][:])
+        nc.scalar.copy(h[:, 2, first], ha_ps[1][:, 0, :])
         hd = sb("hd", [P, PACK, S], F32, tag="zb1")
         for u in range(2):
             pair = slice(2 * u, 2 * u + 2)
@@ -217,20 +235,21 @@ def tile_picked_latecrossbemo_none_po_kernel(
         h3d = sb("h3d", [P, PACK, S], F32)
         res = sb("res", [P, PACK, S], F32)
         out_rows = out_0.rearrange("(p t) n -> p t n", t=PACK)
-        nc.vector.tensor_copy(h[3][:, second], hb_ps[1][:, 1, :])
-        nc.scalar.copy(h[0][:, second], hb_ps[0][:, 0, :])
-        nc.scalar.copy(h[1][:, second], hb_ps[0][:, 1, :])
-        nc.vector.tensor_tensor(hd[:, 2:4, second], hb_ps[1][:], d4[:, 2:4, second], MULT)
-        nc.scalar.activation(h3[:, 0, :], h[0][:].indirect(n3_t[:]), COPY)
-        nc.scalar.copy(h[2][:, second], hb_ps[1][:, 0, :])
-        nc.scalar.activation(h3[:, 1, :], h[1][:].indirect(n3_t[:]), COPY)
-        nc.scalar.activation(h3[:, 2, :], h[2][:].indirect(n3_t[:]), COPY)
-        nc.vector.tensor_tensor(h3d[:, 3, :], h[3][:].indirect(n3_t[:]), ds[:, 3, :], MULT)
-        nc.vector.tensor_tensor(hd[:, 0:2, second], hb_ps[0][:], d4[:, 0:2, second], MULT)
+        nc.vector.tensor_copy(h_last[:, second], hb3_ps[:])
+        nc.vector.tensor_tensor(hd[:, 3, second], hb3_ps[:], d4[:, 3, second], MULT)
+        nc.vector.tensor_tensor(h3d[:, 3, :], h_last[:].indirect(n3_t[:]), ds[:, 3, :], MULT)
+        nc.scalar.copy(h[:, 0:2, second], hb01_ps[:])
+        nc.scalar.activation(h3[:, 0, :], two_rows(h, 0).indirect(n3_t[:]), COPY)
+        nc.scalar.copy(h[:, 2, second], hb2_ps[:])
+        nc.scalar.activation(h3[:, 1, :], two_rows(h, 1).indirect(n3_t[:]), COPY)
+        nc.scalar.activation(h3[:, 2, :], two_rows(h, 2).indirect(n3_t[:]), COPY)
+        nc.vector.tensor_tensor(hd[:, 0:2, second], hb01_ps[:], d4[:, 0:2, second], MULT)
+        nc.vector.tensor_tensor(hd[:, 2, second], hb2_ps[:], d4[:, 2, second], MULT)
         for t in (3, 0, 1, 2):
             if t < 3:
                 nc.vector.tensor_tensor(h3d[:, t, :], h3[:, t, :], ds[:, t, :], MULT)
-            nc.vector.tensor_tensor(res[:, t, :], hd[:, t, :], h3d[:, t, :], SUB)
+            for cols in [slice(0, S)] if t != 2 else [first, second]:
+                nc.vector.tensor_tensor(res[:, t, cols], hd[:, t, cols], h3d[:, t, cols], SUB)
             nc.sync.dma_start(out_rows[:, t, :], res[:, t, :])
 
         o_w = sb("o_w", [P, S], U32)
@@ -238,11 +257,11 @@ def tile_picked_latecrossbemo_none_po_kernel(
         out_words = out_1[0].rearrange("p n t -> p (n t)").bitcast(I32)
         ob = [sb("ob%d" % c, [P, HALF, PACK], BF16) for c in range(2)]
         for c, cols in enumerate((first, second)):
-            nc.vector.tensor_copy(
+            (nc.scalar.copy, nc.vector.tensor_copy)[c](
                 ob[c][:].rearrange("p (a i) t -> p a t i", i=4),
                 res[:, :, cols].rearrange("p t (a i) -> p a t i", i=4),
             )
-        for c, cols in enumerate((first, second)):
+        for c, cols in ((1, second), (0, first)):
             nc.vector.quantize_mx(o_w[:, cols].bitcast(FP8X4), o_s[:, cols], ob[c][:].rearrange("p n t -> p (n t)"))
         nc.sync.dma_start(out_words, o_w[:].bitcast(I32))
         for q in range(4):

@@ -3,7 +3,7 @@ from contextlib import ExitStack
 import concourse.mybir as mybir
 
 K, T, S, N, H = 512, 2048, 256, 512, 512
-FLOPS = 3 * 2 * 512 * 512 * 256
+FLOPS = 2 * S * (K * H + H * N + K * N)
 
 F32 = mybir.dt.float32
 BF16 = mybir.dt.bfloat16
@@ -22,8 +22,11 @@ COPY = mybir.ActivationFunctionType.Copy
 
 P = 128
 PACK = 4
+QUADRANTS = 4
 HALF = S // 2
 LIST_COLS = S // 16
+RUN = 4
+SPARE = 16
 
 
 def tile_picked_latecrossbemo_none_po_kernel(
@@ -38,43 +41,46 @@ def tile_picked_latecrossbemo_none_po_kernel(
         def sb(name, shape, dtype, tag=None):
             return keep.tile(shape, dtype, name=name, tag=tag or name, align_bytes=64)
 
+        def scale_rows(q):
+            return slice(32 * q, 32 * q + 4)
+
         def load_list(name, src):
-            t = keep.tile([P, LIST_COLS], U16, name=name)
-            nc.sync.dma_start(t[:], src)
-            return t
+            tile = keep.tile([P, LIST_COLS], U16, name=name)
+            nc.sync.dma_start(tile[:], src)
+            return tile
 
-        def load_scale_rows(dst, src, quadrants=range(4)):
+        def load_scale_rows(dst, src, quadrants=range(QUADRANTS)):
             for q in quadrants:
-                nc.sync.dma_start(dst[32 * q : 32 * q + 4, :].bitcast(I32), src[0, 4 * q : 4 * q + 4, :].bitcast(I32))
+                nc.sync.dma_start(dst[scale_rows(q), :].bitcast(I32), src[0, 4 * q : 4 * q + 4, :].bitcast(I32))
 
-        def load_words(queue, name, src):
-            t = sb(name, [P, H // 2], I32)
-            queue.dma_start(t[:], src[0].bitcast(I32))
-            return t
+        def load_weight_words(name, src):
+            tile = sb(name, [P, H // 2], I32)
+            nc.sync.dma_start(tile[:], src[0].bitcast(I32))
+            return tile
 
-        def load_rows(name, src):
-            t = sb(name, [P, PACK], F32)
-            nc.gpsimd.dma_start(t[:], src.rearrange("(p t) o -> p (t o)", t=PACK))
-            return t
+        def load_row_values(name, src):
+            tile = sb(name, [P, PACK], F32)
+            nc.gpsimd.dma_start(tile[:], src.rearrange("(p t) o -> p (t o)", t=PACK))
+            return tile
 
         def deal_words(name, raw):
-            t = sb(name, [P, 2 * H], U8)
+            tile = sb(name, [P, 2 * H], U8)
             nc.scalar.copy(
-                t[:].bitcast(U16).rearrange("p (t m) -> p t m", t=PACK),
+                tile[:].bitcast(U16).rearrange("p (t m) -> p t m", t=PACK),
                 raw[:].bitcast(U16).rearrange("p (m t) -> p t m", t=PACK),
             )
-            return t
+            return tile
 
-        def deal_scales(name, raw, engine):
-            t = sb(name, [P, H], U8)
-            engine.tensor_copy(
-                t[:].rearrange("p (t m) -> p t m", t=PACK),
-                raw.rearrange("p (m t) -> p t m", t=PACK),
+        def deal_scales(name, raw):
+            tile = sb(name, [P, H], U8)
+            nc.vector.tensor_copy(
+                tile[:].rearrange("p (t m) -> p t m", t=PACK),
+                raw[:].rearrange("p (m t) -> p t m", t=PACK),
             )
-            return t
+            return tile
 
-        def half_list(lst, c):
-            return lst[:, c * (LIST_COLS // 2) : (c + 1) * (LIST_COLS // 2)]
+        def half_list(tile, c):
+            return tile[:, c * (LIST_COLS // 2) : (c + 1) * (LIST_COLS // 2)]
 
         def two_rows(tile, t):
             return tile[:, t : t + 2, :].rearrange("p t n -> p (t n)")
@@ -107,39 +113,39 @@ def tile_picked_latecrossbemo_none_po_kernel(
         xw = sb("xw", [P, T], I32)
         nc.sync.dma_start(xw[:], x_words[0].rearrange("p n t -> p (n t)").bitcast(I32))
         load_scale_rows(w1s_stage, w1_scales, (2, 3))
-        w1w_raw = load_words(nc.sync, "w1w_raw", w1_words)
+        w1w_raw = load_weight_words("w1w_raw", w1_words)
         two_t = load_list("two_t", two)
         n1_t = load_list("n1_t", n1)
-        w3w_raw = load_words(nc.sync, "w3w_raw", w3_words)
-        w2w_raw = load_words(nc.sync, "w2w_raw", w2_words)
+        w3w_raw = load_weight_words("w3w_raw", w3_words)
+        w2w_raw = load_weight_words("w2w_raw", w2_words)
         n2_t = load_list("n2_t", n2)
-        sl_t = load_rows("sl_t", sl)
-        th_t = load_rows("th_t", th)
-        slth = sb("slth", [P, PACK], F32)
-        nc.gpsimd.tensor_tensor(slth[:], sl_t[:], th_t[:], MULT)
+        sl_t = load_row_values("sl_t", sl)
+        th_t = load_row_values("th_t", th)
+        sl_th = sb("sl_th", [P, PACK], F32)
+        nc.gpsimd.tensor_tensor(sl_th[:], sl_t[:], th_t[:], MULT)
         bias = sb("bias", [P, PACK], F32)
-        nc.gpsimd.tensor_scalar(bias[:], slth[:], -1.0, 0.0, MULT, ADD)
-        gn_t = load_rows("gn_t", gn)
+        nc.gpsimd.tensor_scalar(bias[:], sl_th[:], -1.0, 0.0, MULT, ADD)
+        gn_t = load_row_values("gn_t", gn)
         load_scale_rows(w3s_raw, w3_scales)
         load_scale_rows(w2s_raw, w2_scales)
         n4_t = load_list("n4_t", n4)
         n3_t = load_list("n3_t", n3)
+
         ds = sb("ds", [P, PACK + 1, S], F32)
         nc.vector.memset(ds[:, PACK, :], 0.0)
         h = sb("h", [P, PACK, S], F32)
-        nc.scalar.copy(h[:, PACK - 1, :], ds[:, PACK, :])
-        h_last = sb("h_last", [P, S + 16], F32)
-        nc.scalar.copy(h_last[:, S:], ds[:, PACK, 0:16])
+        nc.scalar.activation(h[:, PACK - 1, :], ds[:, PACK, :], SIGMOID)
+        h_last = sb("h_last", [P, S + SPARE], F32)
+        nc.scalar.activation(h_last[:, S:], ds[:, PACK, 0:SPARE], SIGMOID)
         y = [sb("y%d" % t, [P, 2 * S], F32) for t in range(PACK)]
         for t in range(PACK):
-            nc.scalar.copy(y[t][:, S:], ds[:, PACK, :])
+            nc.scalar.activation(y[t][:, S:], ds[:, PACK, :], SIGMOID)
 
-        for q in range(4):
-            rows = slice(32 * q, 32 * q + 4)
-            nc.vector.tensor_copy(xs[rows, :].bitcast(I32), xs_stage[rows, :].bitcast(I32))
-        for q in range(4):
-            rows = slice(32 * q, 32 * q + 4)
-            nc.scalar.copy(w1s_raw[rows, :].bitcast(U32), w1s_stage[rows, :].bitcast(U32))
+        for q in range(QUADRANTS):
+            nc.vector.tensor_copy(xs[scale_rows(q), :].bitcast(I32), xs_stage[scale_rows(q), :].bitcast(I32))
+        for q in range(QUADRANTS):
+            nc.scalar.copy(w1s_raw[scale_rows(q), :].bitcast(U32), w1s_stage[scale_rows(q), :].bitcast(U32))
+
         xa_s = sb("xa_s", [P, S], U8)
         nc.vector.tensor_copy(xa_s[:], xs[:].indirect(offs_t[:]))
         xa_w = sb("xa_w", [P, S], U32)
@@ -157,7 +163,6 @@ def tile_picked_latecrossbemo_none_po_kernel(
 
         xb_w = sb("xb_w", [P, S], U32)
         nc.vector.tensor_copy(xb_w[:], xw[:].bitcast(U32).indirect(two_t[:]))
-
         for t in range(PACK):
             nc.vector.tensor_copy(y[t][:, 0:S], y_ps[t][:])
 
@@ -165,8 +170,8 @@ def tile_picked_latecrossbemo_none_po_kernel(
         nc.vector.tensor_copy(xb_s[:], xs[:].indirect(two_t[:]))
         w3w = deal_words("w3w", w3w_raw)
         w2w = deal_words("w2w", w2w_raw)
-        w3s = deal_scales("w3s", w3s_raw[:], nc.vector)
-        w2s = deal_scales("w2s", w2s_raw[:], nc.vector)
+        w3s = deal_scales("w3s", w3s_raw)
+        w2s = deal_scales("w2s", w2s_raw)
         d_ps = [psum.tile([P, 2, S], F32, name="d_ps%d" % u, tag="bank%d" % (4 + u)) for u in range(2)]
         for t in range(PACK):
             product(d_ps[t // 2][:, t % 2, :], w3w, w3s, t, xb_w[:], xb_s[:])
@@ -175,19 +180,19 @@ def tile_picked_latecrossbemo_none_po_kernel(
 
         first, second = slice(0, HALF), slice(HALF, S)
         sg = sb("sg", [P, PACK, S], F32, tag="w3w_raw")
-        y2 = sb("y_n2", [P, PACK, S], F32, tag="w2w_raw")
-        ysg = sb("ysg", [P, PACK, S], F32, tag="w3s_raw")
+        y_n2 = sb("y_n2", [P, PACK, S], F32, tag="w2w_raw")
+        y_sg = sb("y_sg", [P, PACK, S], F32, tag="w3s_raw")
         top = sb("top", [P, PACK, S], F32, tag="w3s")
 
         def gate(t):
             nc.scalar.activation(
                 sg[:, t, :], y[t][:].indirect(n1_t[:]), SIGMOID, bias=bias[:, t : t + 1], scale=sl_t[:, t : t + 1]
             )
-            nc.vector.tensor_tensor(ysg[:, t, :], y[t][:, 0:S], sg[:, t, :], MULT)
+            nc.vector.tensor_tensor(y_sg[:, t, :], y[t][:, 0:S], sg[:, t, :], MULT)
 
         def larger(t, offsets, cols):
-            nc.scalar.activation(y2[:, t, cols], y[t][:].indirect(offsets), COPY)
-            nc.vector.scalar_tensor_tensor(top[:, t, cols], y2[:, t, cols], 0.75, ysg[:, t, cols], MULT, MAX)
+            nc.scalar.activation(y_n2[:, t, cols], y[t][:].indirect(offsets), COPY)
+            nc.vector.scalar_tensor_tensor(top[:, t, cols], y_n2[:, t, cols], 0.75, y_sg[:, t, cols], MULT, MAX)
 
         for t in (0, 1):
             gate(t)
@@ -203,14 +208,14 @@ def tile_picked_latecrossbemo_none_po_kernel(
             [(t, ha_ps[t // 2][:, t % 2, :]) for t in range(PACK)],
             [(3, hb3_ps[:]), (0, hb01_ps[:, 0, :]), (1, hb01_ps[:, 1, :]), (2, hb2_ps[:])],
         ]
-        gain = gn_t[:].unsqueeze(1).unsqueeze(3).to_broadcast([P, HALF // 4, PACK, 4])
+        gain = gn_t[:].unsqueeze(1).unsqueeze(3).to_broadcast([P, HALF // RUN, PACK, RUN])
         for c, cols in enumerate((first, second)):
             for t in (2, 3):
                 larger(t, half_list(n2_t, c), cols)
-            zb = sb("zb%d" % c, [P, HALF, PACK], BF16, tag="w2s_raw" if c == 0 else "zb1")
+            zb = sb("zb%d" % c, [P, HALF, PACK], BF16, tag=("w2s_raw", "zb1")[c])
             nc.vector.tensor_tensor(
-                zb[:].rearrange("p (a i) t -> p a t i", i=4),
-                top[:, :, cols].rearrange("p t (a i) -> p a t i", i=4),
+                zb[:].rearrange("p (a i) t -> p a t i", i=RUN),
+                top[:, :, cols].rearrange("p t (a i) -> p a t i", i=RUN),
                 gain,
                 MULT,
             )
@@ -220,37 +225,41 @@ def tile_picked_latecrossbemo_none_po_kernel(
             for t, dst in h_dst[c]:
                 product(dst, w2w, w2s, t, z_w[:], z_s[:])
 
-        d4 = sb("d4", [P, PACK, S], F32)
+        d_n4 = sb("d_n4", [P, PACK, S], F32)
         for t in range(PACK):
-            nc.scalar.activation(d4[:, t, :], two_rows(ds, t).indirect(n4_t[:]), COPY)
+            nc.scalar.activation(d_n4[:, t, :], two_rows(ds, t).indirect(n4_t[:]), COPY)
         nc.vector.tensor_copy(h_last[:, first], ha_ps[1][:, 1, :])
         nc.scalar.copy(h[:, 0:2, first], ha_ps[0][:])
         nc.scalar.copy(h[:, 2, first], ha_ps[1][:, 0, :])
-        hd = sb("hd", [P, PACK, S], F32, tag="zb1")
+        h_dn4 = sb("h_dn4", [P, PACK, S], F32, tag="zb1")
         for u in range(2):
             pair = slice(2 * u, 2 * u + 2)
-            nc.vector.tensor_tensor(hd[:, pair, first], ha_ps[u][:], d4[:, pair, first], MULT)
+            nc.vector.tensor_tensor(h_dn4[:, pair, first], ha_ps[u][:], d_n4[:, pair, first], MULT)
 
-        h3 = sb("h3", [P, PACK - 1, S], F32)
-        h3d = sb("h3d", [P, PACK, S], F32)
+        h_n3 = sb("h_n3", [P, PACK - 1, S], F32)
+        hn3_d = sb("hn3_d", [P, PACK, S], F32)
         res = sb("res", [P, PACK, S], F32)
         out_rows = out_0.rearrange("(p t) n -> p t n", t=PACK)
         nc.vector.tensor_copy(h_last[:, second], hb3_ps[:])
-        nc.vector.tensor_tensor(hd[:, 3, second], hb3_ps[:], d4[:, 3, second], MULT)
-        nc.vector.tensor_tensor(h3d[:, 3, :], h_last[:].indirect(n3_t[:]), ds[:, 3, :], MULT)
+        nc.vector.tensor_tensor(h_dn4[:, 3, second], hb3_ps[:], d_n4[:, 3, second], MULT)
+        nc.vector.tensor_tensor(hn3_d[:, 3, :], h_last[:].indirect(n3_t[:]), ds[:, 3, :], MULT)
         nc.scalar.copy(h[:, 0:2, second], hb01_ps[:])
-        nc.scalar.activation(h3[:, 0, :], two_rows(h, 0).indirect(n3_t[:]), COPY)
+        nc.scalar.activation(h_n3[:, 0, :], two_rows(h, 0).indirect(n3_t[:]), COPY)
         nc.scalar.copy(h[:, 2, second], hb2_ps[:])
-        nc.scalar.activation(h3[:, 1, :], two_rows(h, 1).indirect(n3_t[:]), COPY)
-        nc.scalar.activation(h3[:, 2, :], two_rows(h, 2).indirect(n3_t[:]), COPY)
-        nc.vector.tensor_tensor(hd[:, 0:2, second], hb01_ps[:], d4[:, 0:2, second], MULT)
-        nc.vector.tensor_tensor(hd[:, 2, second], hb2_ps[:], d4[:, 2, second], MULT)
-        for t in (3, 0, 1, 2):
-            if t < 3:
-                nc.vector.tensor_tensor(h3d[:, t, :], h3[:, t, :], ds[:, t, :], MULT)
-            for cols in [slice(0, S)] if t != 2 else [first, second]:
-                nc.vector.tensor_tensor(res[:, t, cols], hd[:, t, cols], h3d[:, t, cols], SUB)
+        nc.scalar.activation(h_n3[:, 1, :], two_rows(h, 1).indirect(n3_t[:]), COPY)
+        nc.scalar.activation(h_n3[:, 2, :], two_rows(h, 2).indirect(n3_t[:]), COPY)
+        nc.vector.tensor_tensor(h_dn4[:, 0:2, second], hb01_ps[:], d_n4[:, 0:2, second], MULT)
+        nc.vector.tensor_tensor(h_dn4[:, 2, second], hb2_ps[:], d_n4[:, 2, second], MULT)
+
+        def subtract_and_store(t, pieces):
+            for cols in pieces:
+                nc.vector.tensor_tensor(res[:, t, cols], h_dn4[:, t, cols], hn3_d[:, t, cols], SUB)
             nc.sync.dma_start(out_rows[:, t, :], res[:, t, :])
+
+        subtract_and_store(3, [slice(0, S)])
+        for t, pieces in ((0, [slice(0, S)]), (1, [slice(0, S)]), (2, [first, second])):
+            nc.vector.tensor_tensor(hn3_d[:, t, :], h_n3[:, t, :], ds[:, t, :], MULT)
+            subtract_and_store(t, pieces)
 
         o_w = sb("o_w", [P, S], U32)
         o_s = sb("o_s", [P, S], U8)
@@ -258,12 +267,12 @@ def tile_picked_latecrossbemo_none_po_kernel(
         ob = [sb("ob%d" % c, [P, HALF, PACK], BF16) for c in range(2)]
         for c, cols in enumerate((first, second)):
             (nc.scalar.copy, nc.vector.tensor_copy)[c](
-                ob[c][:].rearrange("p (a i) t -> p a t i", i=4),
-                res[:, :, cols].rearrange("p t (a i) -> p a t i", i=4),
+                ob[c][:].rearrange("p (a i) t -> p a t i", i=RUN),
+                res[:, :, cols].rearrange("p t (a i) -> p a t i", i=RUN),
             )
         for c, cols in ((1, second), (0, first)):
             nc.vector.quantize_mx(o_w[:, cols].bitcast(FP8X4), o_s[:, cols], ob[c][:].rearrange("p n t -> p (n t)"))
-        nc.sync.dma_start(out_words, o_w[:].bitcast(I32))
-        for q in range(4):
-            queue = nc.sync if q % 2 == 1 else nc.scalar
-            queue.dma_start(out_2[0, 4 * q : 4 * q + 4, :].bitcast(I32), o_s[32 * q : 32 * q + 4, :].bitcast(I32))
+            nc.sync.dma_start(out_words[:, cols], o_w[:, cols].bitcast(I32))
+        for q in range(QUADRANTS):
+            queue = (nc.scalar, nc.sync)[q % 2]
+            queue.dma_start(out_2[0, 4 * q : 4 * q + 4, :].bitcast(I32), o_s[scale_rows(q), :].bitcast(I32))

from contextlib import ExitStack

import concourse.mybir as mybir

K, T, S, N, H = 512, 2048, 256, 512, 512
FLOPS = 2 * S * (K * H + H * N + K * N)

F32 = mybir.dt.float32
BF16 = mybir.dt.bfloat16
I32 = mybir.dt.int32
U32 = mybir.dt.uint32
U16 = mybir.dt.uint16
U8 = mybir.dt.uint8
FP8X4 = mybir.dt.float8_e4m3fn_x4
FP4X4 = mybir.dt.float4_e2m1fn_x4
MULT = mybir.AluOpType.mult
ADD = mybir.AluOpType.add
MAX = mybir.AluOpType.max
SUB = mybir.AluOpType.subtract
SIGMOID = mybir.ActivationFunctionType.Sigmoid
COPY = mybir.ActivationFunctionType.Copy

P = 128
PACK = 4
QUADRANTS = 4
HALF = S // 2
LIST_COLS = S // 16
RUN = 4
SPARE = 16


def tile_picked_latecrossbemo_none_po_kernel(
    tc, x_words, x_scales, w1_words, w1_scales, sl, th, gn, w2_words, w2_scales, w3_words, w3_scales,
    offs, n1, n2, two, n3, n4, out_0, out_1, out_2,
):
    nc = tc.nc
    with ExitStack() as ctx:
        keep = ctx.enter_context(tc.tile_pool(name="keep", bufs=1))
        psum = ctx.enter_context(tc.psum_pool(name="psum", bufs=1))

        def sb(name, shape, dtype, tag=None):
            return keep.tile(shape, dtype, name=name, tag=tag or name, align_bytes=64)

        def scale_rows(q):
            return slice(32 * q, 32 * q + 4)

        def load_list(name, src):
            tile = keep.tile([P, LIST_COLS], U16, name=name)
            nc.sync.dma_start(tile[:], src)
            return tile

        def load_scale_rows(dst, src, quadrants=range(QUADRANTS)):
            for q in quadrants:
                nc.sync.dma_start(dst[scale_rows(q), :].bitcast(I32), src[0, 4 * q : 4 * q + 4, :].bitcast(I32))

        def load_weight_words(name, src):
            tile = sb(name, [P, H // 2], I32)
            nc.sync.dma_start(tile[:], src[0].bitcast(I32))
            return tile

        def load_row_values(name, src):
            tile = sb(name, [P, PACK], F32)
            nc.gpsimd.dma_start(tile[:], src.rearrange("(p t) o -> p (t o)", t=PACK))
            return tile

        def deal_words(name, raw):
            tile = sb(name, [P, 2 * H], U8)
            nc.scalar.copy(
                tile[:].bitcast(U16).rearrange("p (t m) -> p t m", t=PACK),
                raw[:].bitcast(U16).rearrange("p (m t) -> p t m", t=PACK),
            )
            return tile

        def deal_scales(name, raw):
            tile = sb(name, [P, H], U8)
            nc.vector.tensor_copy(
                tile[:].rearrange("p (t m) -> p t m", t=PACK),
                raw[:].rearrange("p (m t) -> p t m", t=PACK),
            )
            return tile

        def half_list(tile, c):
            return tile[:, c * (LIST_COLS // 2) : (c + 1) * (LIST_COLS // 2)]

        def two_rows(tile, t):
            return tile[:, t : t + 2, :].rearrange("p t n -> p (t n)")

        def product(out, words, scales, t, rhs_words, rhs_scales):
            nc.tensor.matmul_mx(
                out=out,
                lhsT=words[:, 2 * P * t : 2 * P * (t + 1)].bitcast(FP4X4),
                lhsT_scale=scales[:, P * t : P * (t + 1)],
                rhs=rhs_words.bitcast(FP8X4),
                rhs_scale=rhs_scales,
                start=True,
                stop=True,
            )

        xs = sb("xs", [P, T], U8)
        nc.vector.memset(xs[:].bitcast(I32), 0)
        w1s_raw = sb("w1s_raw", [P, H], U8)
        nc.vector.memset(w1s_raw[:].bitcast(I32), 0)
        w3s_raw = sb("w3s_raw", [P, N], U8)
        w2s_raw = sb("w2s_raw", [P, N], U8)
        nc.vector.memset(w3s_raw[:].bitcast(I32), 0)
        nc.vector.memset(w2s_raw[:].bitcast(I32), 0)

        xs_stage = sb("xs_stage", [P, T], U8)
        w1s_stage = sb("w1s_stage", [P, H], U8)
        load_scale_rows(xs_stage, x_scales)
        offs_t = load_list("offs_t", offs)
        load_scale_rows(w1s_stage, w1_scales, (0, 1))
        xw = sb("xw", [P, T], I32)
        nc.sync.dma_start(xw[:], x_words[0].rearrange("p n t -> p (n t)").bitcast(I32))
        load_scale_rows(w1s_stage, w1_scales, (2, 3))
        w1w_raw = load_weight_words("w1w_raw", w1_words)
        two_t = load_list("two_t", two)
        n1_t = load_list("n1_t", n1)
        w3w_raw = load_weight_words("w3w_raw", w3_words)
        w2w_raw = load_weight_words("w2w_raw", w2_words)
        n2_t = load_list("n2_t", n2)
        sl_t = load_row_values("sl_t", sl)
        th_t = load_row_values("th_t", th)
        sl_th = sb("sl_th", [P, PACK], F32)
        nc.gpsimd.tensor_tensor(sl_th[:], sl_t[:], th_t[:], MULT)
        bias = sb("bias", [P, PACK], F32)
        nc.gpsimd.tensor_scalar(bias[:], sl_th[:], -1.0, 0.0, MULT, ADD)
        gn_t = load_row_values("gn_t", gn)
        load_scale_rows(w3s_raw, w3_scales)
        load_scale_rows(w2s_raw, w2_scales)
        n4_t = load_list("n4_t", n4)
        n3_t = load_list("n3_t", n3)

        ds = sb("ds", [P, PACK + 1, S], F32)
        nc.vector.memset(ds[:, PACK, :], 0.0)
        h = sb("h", [P, PACK, S], F32)
        nc.scalar.activation(h[:, PACK - 1, :], ds[:, PACK, :], SIGMOID)
        h_last = sb("h_last", [P, S + SPARE], F32)
        nc.scalar.activation(h_last[:, S:], ds[:, PACK, 0:SPARE], SIGMOID)
        y = [sb("y%d" % t, [P, 2 * S], F32) for t in range(PACK)]
        for t in range(PACK):
            nc.scalar.activation(y[t][:, S:], ds[:, PACK, :], SIGMOID)

        for q in range(QUADRANTS):
            nc.vector.tensor_copy(xs[scale_rows(q), :].bitcast(I32), xs_stage[scale_rows(q), :].bitcast(I32))
        for q in range(QUADRANTS):
            nc.scalar.copy(w1s_raw[scale_rows(q), :].bitcast(U32), w1s_stage[scale_rows(q), :].bitcast(U32))

        xa_s = sb("xa_s", [P, S], U8)
        nc.vector.tensor_copy(xa_s[:], xs[:].indirect(offs_t[:]))
        xa_w = sb("xa_w", [P, S], U32)
        nc.vector.tensor_copy(xa_w[:], xw[:].bitcast(U32).indirect(offs_t[:]))
        w1s = sb("w1s", [P, H], U8)
        for t in range(PACK):
            nc.vector.tensor_copy(w1s[:, P * t : P * (t + 1)], w1s_raw[:, t:H:PACK])
        w1w = sb("w1w", [P, 2 * H], U8)
        for t in range(PACK):
            nc.scalar.copy(w1w[:, 2 * P * t : 2 * P * (t + 1)].bitcast(U16), w1w_raw[:].bitcast(U16)[:, t:H:PACK])

        y_ps = [psum.tile([P, S], F32, name="y_ps%d" % t, tag="bank%d" % t) for t in range(PACK)]
        for t in range(PACK):
            product(y_ps[t][:], w1w, w1s, t, xa_w[:], xa_s[:])

        xb_w = sb("xb_w", [P, S], U32)
        nc.vector.tensor_copy(xb_w[:], xw[:].bitcast(U32).indirect(two_t[:]))
        for t in range(PACK):
            nc.vector.tensor_copy(y[t][:, 0:S], y_ps[t][:])

        xb_s = sb("xb_s", [P, S], U8)
        nc.vector.tensor_copy(xb_s[:], xs[:].indirect(two_t[:]))
        w3w = deal_words("w3w", w3w_raw)
        w2w = deal_words("w2w", w2w_raw)
        w3s = deal_scales("w3s", w3s_raw)
        w2s = deal_scales("w2s", w2s_raw)
        d_ps = [psum.tile([P, 2, S], F32, name="d_ps%d" % u, tag="bank%d" % (4 + u)) for u in range(2)]
        for t in range(PACK):
            product(d_ps[t // 2][:, t % 2, :], w3w, w3s, t, xb_w[:], xb_s[:])
        for u in range(2):
            nc.vector.tensor_scalar(ds[:, 2 * u : 2 * u + 2, :], d_ps[u][:], 0.75, None, MULT)

        first, second = slice(0, HALF), slice(HALF, S)
        sg = sb("sg", [P, PACK, S], F32, tag="w3w_raw")
        y_n2 = sb("y_n2", [P, PACK, S], F32, tag="w2w_raw")
        y_sg = sb("y_sg", [P, PACK, S], F32, tag="w3s_raw")
        top = sb("top", [P, PACK, S], F32, tag="w3s")

        def gate(t):
            nc.scalar.activation(
                sg[:, t, :], y[t][:].indirect(n1_t[:]), SIGMOID, bias=bias[:, t : t + 1], scale=sl_t[:, t : t + 1]
            )
            nc.vector.tensor_tensor(y_sg[:, t, :], y[t][:, 0:S], sg[:, t, :], MULT)

        def larger(t, offsets, cols):
            nc.scalar.activation(y_n2[:, t, cols], y[t][:].indirect(offsets), COPY)
            nc.vector.scalar_tensor_tensor(top[:, t, cols], y_n2[:, t, cols], 0.75, y_sg[:, t, cols], MULT, MAX)

        for t in (0, 1):
            gate(t)
            larger(t, n2_t[:], slice(0, S))
        for t in (2, 3):
            gate(t)

        ha_ps = [psum.tile([P, 2, HALF], F32, name="ha_ps%d" % u, tag="bank%d" % (4 + u)) for u in range(2)]
        hb01_ps = psum.tile([P, 2, HALF], F32, name="hb01_ps", tag="bank6")
        hb2_ps = psum.tile([P, HALF], F32, name="hb2_ps", tag="bank7")
        hb3_ps = psum.tile([P, HALF], F32, name="hb3_ps", tag="bank0")
        h_dst = [
            [(t, ha_ps[t // 2][:, t % 2, :]) for t in range(PACK)],
            [(3, hb3_ps[:]), (0, hb01_ps[:, 0, :]), (1, hb01_ps[:, 1, :]), (2, hb2_ps[:])],
        ]
        gain = gn_t[:].unsqueeze(1).unsqueeze(3).to_broadcast([P, HALF // RUN, PACK, RUN])
        for c, cols in enumerate((first, second)):
            for t in (2, 3):
                larger(t, half_list(n2_t, c), cols)
            zb = sb("zb%d" % c, [P, HALF, PACK], BF16, tag=("w2s_raw", "zb1")[c])
            nc.vector.tensor_tensor(
                zb[:].rearrange("p (a i) t -> p a t i", i=RUN),
                top[:, :, cols].rearrange("p t (a i) -> p a t i", i=RUN),
                gain,
                MULT,
            )
            z_w = sb("z_w%d" % c, [P, HALF], U32)
            z_s = sb("z_s%d" % c, [P, HALF], U8)
            nc.vector.quantize_mx(z_w[:].bitcast(FP8X4), z_s[:], zb[:].rearrange("p n t -> p (n t)"))
            for t, dst in h_dst[c]:
                product(dst, w2w, w2s, t, z_w[:], z_s[:])

        d_n4 = sb("d_n4", [P, PACK, S], F32)
        for t in range(PACK):
            nc.scalar.activation(d_n4[:, t, :], two_rows(ds, t).indirect(n4_t[:]), COPY)
        nc.vector.tensor_copy(h_last[:, first], ha_ps[1][:, 1, :])
        nc.scalar.copy(h[:, 0:2, first], ha_ps[0][:])
        nc.scalar.copy(h[:, 2, first], ha_ps[1][:, 0, :])
        h_dn4 = sb("h_dn4", [P, PACK, S], F32, tag="zb1")
        for u in range(2):
            pair = slice(2 * u, 2 * u + 2)
            nc.vector.tensor_tensor(h_dn4[:, pair, first], ha_ps[u][:], d_n4[:, pair, first], MULT)

        h_n3 = sb("h_n3", [P, PACK - 1, S], F32)
        hn3_d = sb("hn3_d", [P, PACK, S], F32)
        res = sb("res", [P, PACK, S], F32)
        out_rows = out_0.rearrange("(p t) n -> p t n", t=PACK)
        nc.vector.tensor_copy(h_last[:, second], hb3_ps[:])
        nc.vector.tensor_tensor(h_dn4[:, 3, second], hb3_ps[:], d_n4[:, 3, second], MULT)
        nc.vector.tensor_tensor(hn3_d[:, 3, :], h_last[:].indirect(n3_t[:]), ds[:, 3, :], MULT)
        nc.scalar.copy(h[:, 0:2, second], hb01_ps[:])
        nc.scalar.activation(h_n3[:, 0, :], two_rows(h, 0).indirect(n3_t[:]), COPY)
        nc.scalar.copy(h[:, 2, second], hb2_ps[:])
        nc.scalar.activation(h_n3[:, 1, :], two_rows(h, 1).indirect(n3_t[:]), COPY)
        nc.scalar.activation(h_n3[:, 2, :], two_rows(h, 2).indirect(n3_t[:]), COPY)
        nc.vector.tensor_tensor(h_dn4[:, 0:2, second], hb01_ps[:], d_n4[:, 0:2, second], MULT)
        nc.vector.tensor_tensor(h_dn4[:, 2, second], hb2_ps[:], d_n4[:, 2, second], MULT)

        def subtract_and_store(t, pieces):
            for cols in pieces:
                nc.vector.tensor_tensor(res[:, t, cols], h_dn4[:, t, cols], hn3_d[:, t, cols], SUB)
            nc.sync.dma_start(out_rows[:, t, :], res[:, t, :])

        subtract_and_store(3, [slice(0, S)])
        for t, pieces in ((0, [slice(0, S)]), (1, [slice(0, S)]), (2, [first, second])):
            nc.vector.tensor_tensor(hn3_d[:, t, :], h_n3[:, t, :], ds[:, t, :], MULT)
            subtract_and_store(t, pieces)

        o_w = sb("o_w", [P, S], U32)
        o_s = sb("o_s", [P, S], U8)
        out_words = out_1[0].rearrange("p n t -> p (n t)").bitcast(I32)
        ob = [sb("ob%d" % c, [P, HALF, PACK], BF16) for c in range(2)]
        for c, cols in enumerate((first, second)):
            (nc.scalar.copy, nc.vector.tensor_copy)[c](
                ob[c][:].rearrange("p (a i) t -> p a t i", i=RUN),
                res[:, :, cols].rearrange("p t (a i) -> p a t i", i=RUN),
            )
        for c, cols in ((1, second), (0, first)):
            nc.vector.quantize_mx(o_w[:, cols].bitcast(FP8X4), o_s[:, cols], ob[c][:].rearrange("p n t -> p (n t)"))
            nc.sync.dma_start(out_words[:, cols], o_w[:, cols].bitcast(I32))
        for q in range(QUADRANTS):
            queue = (nc.scalar, nc.sync)[q % 2]
            queue.dma_start(out_2[0, 4 * q : 4 * q + 4, :].bitcast(I32), o_s[scale_rows(q), :].bitcast(I32))
